import numpy as np
import ml_dtypes


def mxq(x, axis, fmt="e4m3"):
    dtype, down = {"e4m3": (ml_dtypes.float8_e4m3fn, 7), "e5m2": (ml_dtypes.float8_e5m2, 14)}[fmt]
    v = np.moveaxis(np.asarray(x, np.float32).astype(ml_dtypes.bfloat16).astype(np.float64), axis, -1)
    blocks = v.reshape(v.shape[:-1] + (-1, 32))
    amax = np.abs(blocks).max(-1, keepdims=True)
    byte = np.maximum(np.where(amax > 0, np.frexp(amax)[1] - 1 + 127, 0) - down, 1)
    scale = np.exp2(byte - 127.0)
    codes = (blocks / scale).astype(np.float32).astype(dtype).astype(np.float64)
    return np.moveaxis((codes * scale).reshape(v.shape), -1, axis)


WIDE = False


def mx_kscale(k):
    if not WIDE:
        return np.ones(k)
    levels = np.array([10, -10, 5, -5, 0])
    if k % 512:
        return np.exp2(np.random.permutation(np.resize(levels, k // 32))).repeat(32)
    a = np.empty((k // 512, 16))
    for p in range(k // 512):
        a[p, :8] = np.random.permutation(np.resize(levels, 8))
        for g in range(8):
            far = levels[np.abs(levels - a[p, g]) >= 10]
            a[p, g + 8] = far[np.random.randint(len(far))]
    return np.exp2(a.ravel()).repeat(32)


def f64(x):
    return np.asarray(x).astype(np.float64)


def striped(idx):
    return np.tile(idx.reshape(-1, 16).T, (8, 1)).astype(np.uint16)


def unstriped(offs):
    return offs[:16].T.reshape(-1).astype(np.int64)


def pack_weight(w):
    k, n = w.shape
    w = f64(np.asarray(w, np.float32).astype(ml_dtypes.bfloat16)).reshape(k // 32, 32, n)
    amax = np.abs(w).max(1)
    byte = np.clip(np.where(amax > 0, np.frexp(amax)[1] - 1 + 127 - 7, 1), 1, 254)
    scaled = (w * np.exp2(127.0 - byte)[:, None, :]).reshape(k, n).astype(np.float32)
    words = np.ascontiguousarray(scaled.reshape(k // 512, 128, 4, n).transpose(0, 1, 3, 2)).astype(ml_dtypes.float8_e4m3fn).view(np.uint8)
    return words, np.ascontiguousarray(byte.astype(np.uint8).reshape(k // 512, 16, n))


def unpack_weight(words, scales):
    g, p, n, _ = words.shape
    vals = np.ascontiguousarray(words).view(ml_dtypes.float8_e4m3fn).astype(np.float64) * np.repeat(np.exp2(scales.astype(np.float64) - 127.0), 8, axis=1)[..., None]
    return vals.transpose(0, 1, 3, 2).reshape(g * 512, n)


def sigmoid(v):
    return 1.0 / (1.0 + np.exp(-np.maximum(v, -700.0)))


K, T, S, N, H = 512, 1024, 512, 256, 512


def setup_inputs():
    n = np.random.standard_normal
    s = mx_kscale(K)[:, None]
    u = mx_kscale(H)
    packed_xT = pack_weight(n((K, T)) * s)
    return {
        "x_words": packed_xT[0],
        "x_scales": packed_xT[1],
        "w1": (n((K, H)) / np.sqrt(K) / s).astype(np.float32),
        "w2": (n((K, H)) / np.sqrt(K) / s).astype(np.float32),
        "aa": (np.random.uniform(0.1, 0.3, (H, S))).astype(np.float32),
        "cap": (np.random.uniform(0.6, 1.0, (H, S))).astype(np.float32),
        "unit": (np.random.uniform(0.6, 1.4, (H, 1)) * u[:, None]).astype(np.float32),
        "w3": (n((H, N)) / np.sqrt(H) / u[:, None]).astype(np.float32),
        "offs": striped(np.random.permutation(T)[:S]),
        "shl": striped(np.random.permutation(S)),
    }


def reference(x_words, x_scales, w1, w2, aa, cap, unit, w3, offs, shl):
    xq = unpack_weight(x_words, x_scales)[:, unstriped(offs)]
    po = mxq(f64(w1), 0, "e4m3").T @ xq
    por = 0.4 * sigmoid(po) + 0.05
    rt = mxq(f64(w2), 0, "e4m3").T @ xq
    rs = rt[:, unstriped(shl)]
    vsh = sigmoid(rs - rt)
    ff = f64(aa) / ((por) ** 2)
    cond = (-1.0 * vsh + 1.0) / ff + 0.5 * vsh
    res = np.log(np.exp(rt) + 1.0) + 0.2
    sw = np.sqrt(cond / (cond * res + 0.1) + 0.02)
    hid = f64(unit) * ((por * (-1.0 * (np.minimum(sw, f64(cap))) + 1.0)) * ((-1.0 * vsh + 1.0) ** 2))
    return mxq(f64(w3), 0, "e4m3").T @ mxq(hid, 0, "e4m3")

@@ -1,0 +1,204 @@
+from contextlib import ExitStack
+
+import concourse.mybir as mybir
+
+K, T, S, N, H = 512, 1024, 512, 256, 512
+FLOPS = 2 * K * H * S * 2 + 2 * H * N * S
+
+F32 = mybir.dt.float32
+BF16 = mybir.dt.bfloat16
+I32 = mybir.dt.int32
+U32 = mybir.dt.uint32
+U16 = mybir.dt.uint16
+U8 = mybir.dt.uint8
+FP8X4 = mybir.dt.float8_e4m3fn_x4
+ALU = mybir.AluOpType
+ACT = mybir.ActivationFunctionType
+
+P = 128
+PACK = 4
+CHUNK = 128
+LN_FLOOR = 1e-19
+LEAD = 64
+LAG = 2
+SQUARES_ON_VECTOR = 2
+
+
+def tile_picked_yarchi_pay_p_kernel(tc, x_words, x_scales, w1, w2, aa, cap, unit, w3, offs, shl, out):
+    nc = tc.nc
+    with ExitStack() as ctx:
+        keep = ctx.enter_context(tc.tile_pool(name="keep", bufs=1))
+        work = ctx.enter_context(tc.tile_pool(name="work", bufs=4))
+        psum = ctx.enter_context(tc.psum_pool(name="psum", bufs=1))
+
+        offs_sb = keep.tile([P, S // 16], U16, name="offs_sb")
+        shl_sb = keep.tile([P, S // 16], U16, name="shl_sb")
+        xw = keep.tile([P, T], U32, name="xw", align_bytes=64)
+        xs = keep.tile([P, T], U8, name="xs", align_bytes=64)
+        nc.vector.memset(xs[:].bitcast(I32), 0)
+        nc.sync.dma_start(offs_sb[:], offs)
+        for quad in range(4):
+            nc.sync.dma_start(xs[32 * quad : 32 * quad + 4, :].bitcast(I32), x_scales[0, 4 * quad : 4 * quad + 4, :].bitcast(I32))
+        nc.sync.dma_start(xw[:].bitcast(I32), x_words[0].rearrange("p n r -> p (n r)").bitcast(I32))
+
+        def load_halves(w, name):
+            rows = w.rearrange("(p j) c -> p j c", j=PACK)
+            halves = []
+            for h in range(2):
+                raw = keep.tile([P, PACK, H // 2], F32, name=name + str(h))
+                nc.sync.dma_start(raw[:], rows[:, :, h * (H // 2) : (h + 1) * (H // 2)])
+                halves.append(raw)
+            return halves
+
+        w2_raw = load_halves(w2, "w2_raw")
+        w1_raw = load_halves(w1, "w1_raw")
+        nc.sync.dma_start(shl_sb[:], shl)
+        unit_sb = keep.tile([P, PACK], F32, name="unit_sb")
+        nc.sync.dma_start(unit_sb[:], unit.rearrange("(p t) o -> p (t o)", t=PACK))
+        aa_sb = keep.tile([P, PACK, S], F32, name="aa_sb")
+        nc.sync.dma_start(aa_sb[:], aa.rearrange("(p t) j -> p t j", t=PACK))
+        cap_sb = keep.tile([P, PACK, S], F32, name="cap_sb")
+        nc.sync.dma_start(cap_sb[:], cap.rearrange("(p t) j -> p t j", t=PACK))
+        w3_raw = keep.tile([P, PACK, N], F32, name="w3_raw")
+        nc.sync.dma_start(w3_raw[:], w3.rearrange("(p t) m -> p t m", t=PACK))
+
+        x_bytes = keep.tile([P, S], U8, name="x_bytes", align_bytes=64)
+        x_codes = keep.tile([P, S], U32, name="x_codes", align_bytes=64)
+        nc.vector.tensor_copy(x_bytes[:], xs[:].indirect(offs_sb[:]))
+        nc.vector.tensor_copy(x_codes[:], xw[:].indirect(offs_sb[:]))
+
+        def first_product(raw, name):
+            grouped = keep.tile([P, PACK, P, PACK], BF16, name=name + "_grouped", align_bytes=64)
+            for h in range(2):
+                nc.vector.tensor_copy(
+                    grouped[:, :, h * 64 : (h + 1) * 64, :].rearrange("p t m j -> p m t j"),
+                    raw[h][:].rearrange("p j (m t) -> p m t j", t=PACK),
+                )
+            banks = []
+            for t in range(PACK):
+                codes = keep.tile([P, P], U32, name=name + "_codes" + str(t), align_bytes=64)
+                scales = keep.tile([P, P], U8, name=name + "_scales" + str(t), align_bytes=64)
+                nc.vector.quantize_mx(codes[:].bitcast(FP8X4), scales[:], grouped[:, t].rearrange("p m j -> p (m j)"))
+                bank = psum.tile([P, S], F32, name=name + str(t), tag=name + str(t))
+                nc.tensor.matmul_mx(
+                    bank[:], lhsT=codes[:].bitcast(FP8X4), lhsT_scale=scales[:],
+                    rhs=x_codes[:].bitcast(FP8X4), rhs_scale=x_bytes[:], start=True, stop=True,
+                )
+                banks.append(bank)
+            return banks
+
+        rt_banks = first_product(w2_raw, "rt")
+        sg = keep.tile([P, PACK, S], F32, name="sg")
+        nc.scalar.activation(sg[:, 0, :LEAD], rt_banks[0][:, :LEAD], ACT.Sigmoid, scale=-1.0)
+        windows = []
+        for t in range(PACK):
+            window = keep.tile([P, S], F32, name="window" + str(t))
+            nc.scalar.copy(window[:], rt_banks[t][:])
+            windows.append(window)
+
+        po_banks = first_product(w1_raw, "po")
+
+        rt = keep.tile([P, PACK, S], F32, name="rt_sb")
+        diff = keep.tile([P, PACK, S], F32, name="diff")
+        for t in range(PACK):
+            nc.vector.tensor_copy(rt[:, t, :], windows[t][:])
+            for h in range(2):
+                cols = slice(h * 256, (h + 1) * 256)
+                nc.vector.tensor_tensor(diff[:, t, cols], windows[t][:].indirect(shl_sb[:, h * 16 : (h + 1) * 16]), rt[:, t, cols], ALU.subtract)
+
+        sig = keep.tile([P, PACK, S], F32, name="sig")
+        sand = keep.tile([P, PACK, S], F32, name="sand")
+        for t in range(PACK):
+            nc.scalar.activation(sig[:, t, :], po_banks[t][:], ACT.Sigmoid)
+        for t in range(PACK):
+            first = LEAD if t == 0 else 0
+            nc.scalar.activation(sg[:, t, first:], rt_banks[t][:, first:], ACT.Sigmoid, scale=-1.0)
+        for t in range(PACK):
+            nc.scalar.activation(sand[:, t, :], diff[:, t, :], ACT.Sigmoid, scale=-1.0)
+
+        nc.scalar.activation(diff[:], sg[:], ACT.Ln, bias=LN_FLOOR)
+
+        gain = keep.tile([P, PACK], F32, name="gain")
+        nc.vector.tensor_scalar(gain[:], unit_sb[:], -0.4, None, ALU.mult)
+        outer = keep.tile([P, PACK, S], F32, name="outer")
+        zs = []
+        for t in range(PACK):
+            z = work.tile([P, S], F32, name="z")
+            nc.vector.scalar_tensor_tensor(z[:], sig[:, t, :], 0.125, sand[:, t, :], ALU.add, ALU.mult)
+            zs.append(z)
+        for t in range(PACK):
+            nc.vector.scalar_tensor_tensor(outer[:, t, :], zs[t][:], gain[:, t : t + 1], sand[:, t, :], ALU.mult, ALU.mult)
+
+        w3_grouped = keep.tile([P, N, PACK], BF16, name="w3_grouped", align_bytes=64)
+        nc.vector.tensor_copy(
+            w3_grouped[:].rearrange("p (c i) t -> p c t i", i=4),
+            w3_raw[:].rearrange("p t (c i) -> p c t i", i=4),
+        )
+        w3_codes = keep.tile([P, N], U32, name="w3_codes", align_bytes=64)
+        w3_scales = keep.tile([P, N], U8, name="w3_scales", align_bytes=64)
+        nc.vector.quantize_mx(w3_codes[:].bitcast(FP8X4), w3_scales[:], w3_grouped[:].rearrange("p m t -> p (m t)"))
+
+        out_rows = out.rearrange("(b m) j -> m b j", m=P)
+
+        def chunk_steps(c):
+            cols = slice(c * CHUNK, (c + 1) * CHUNK)
+            soft = work.tile([P, PACK, CHUNK], F32, name="soft")
+            x0 = work.tile([P, PACK, CHUNK], F32, name="x0")
+            x1 = work.tile([P, PACK, CHUNK], F32, name="x1")
+            x2 = work.tile([P, PACK, CHUNK], F32, name="x2")
+            rc = work.tile([P, PACK, CHUNK], F32, name="rc")
+            g = work.tile([P, PACK, CHUNK], F32, name="g")
+            rp = work.tile([P, PACK, CHUNK], F32, name="rp")
+            sw = work.tile([P, PACK, CHUNK], F32, name="sw")
+            room = work.tile([P, PACK, CHUNK], F32, name="room")
+            hid = work.tile([P, CHUNK, PACK], BF16, name="hid", align_bytes=64)
+            hid_codes = work.tile([P, CHUNK], U32, name="hid_codes", align_bytes=64)
+            hid_scales = work.tile([P, CHUNK], U8, name="hid_scales", align_bytes=64)
+            acc = psum.tile([P, N // P, CHUNK], F32, name="acc", tag="po" + str(c))
+            res = work.tile([P, N // P, CHUNK], F32, name="res")
+
+            def square_rc():
+                if c < SQUARES_ON_VECTOR:
+                    nc.vector.tensor_tensor(rc[:], rc[:], rc[:], ALU.mult)
+                else:
+                    nc.scalar.activation(rc[:], rc[:], ACT.Square)
+
+            def last_product():
+                for b in range(N // P):
+                    nc.tensor.matmul_mx(
+                        acc[:, b, :], lhsT=w3_codes[:, b * P : (b + 1) * P].bitcast(FP8X4), lhsT_scale=w3_scales[:, b * P : (b + 1) * P],
+                        rhs=hid_codes[:].bitcast(FP8X4), rhs_scale=hid_scales[:], start=True, stop=True,
+                    )
+
+            return [
+                lambda: nc.scalar.activation(sg[:, :, cols], aa_sb[:, :, cols], ACT.Abs_reciprocal_sqrt),
+                lambda: nc.vector.scalar_tensor_tensor(x0[:], sig[:, :, cols], 0.125, sg[:, :, cols], ALU.add, ALU.mult),
+                lambda: nc.scalar.activation(x1[:], x0[:], ACT.Square, scale=0.4),
+                lambda: nc.vector.scalar_tensor_tensor(x2[:], x1[:], -0.5, sand[:, :, cols], ALU.add, ALU.mult),
+                lambda: nc.scalar.activation(rc[:], x2[:], ACT.Abs_reciprocal_sqrt, scale=10.0, bias=5.0),
+                square_rc,
+                lambda: nc.vector.scalar_tensor_tensor(soft[:], diff[:, :, cols], -1.0, rt[:, :, cols], ALU.mult, ALU.max),
+                lambda: nc.vector.scalar_tensor_tensor(g[:], rc[:], 0.2, soft[:], ALU.add, ALU.add),
+                lambda: nc.scalar.activation(rp[:], g[:], ACT.Square, bias=25.0),
+                lambda: nc.scalar.activation(rp[:], rp[:], ACT.Abs_reciprocal_sqrt, scale=50.0, bias=-31250.0),
+                lambda: nc.vector.tensor_scalar(room[:], cap_sb[:, :, cols], -1.0, None, ALU.add),
+                lambda: nc.vector.scalar_tensor_tensor(sw[:], g[:], 50.0, rp[:], ALU.add, ALU.mult),
+                lambda: nc.vector.scalar_tensor_tensor(sw[:], sw[:], -1.0, room[:], ALU.add, ALU.min),
+                lambda: nc.vector.tensor_tensor(
+                    hid[:].rearrange("p (c i) t -> p c t i", i=4),
+                    sw[:].rearrange("p t (c i) -> p c t i", i=4),
+                    outer[:, :, cols].rearrange("p t (c i) -> p c t i", i=4),
+                    ALU.mult,
+                ),
+                lambda: nc.vector.quantize_mx(hid_codes[:].bitcast(FP8X4), hid_scales[:], hid[:].rearrange("p j t -> p (j t)")),
+                last_product,
+                lambda: nc.scalar.copy(res[:], acc[:]),
+                lambda: nc.sync.dma_start(out_rows[:, :, cols], res[:]),
+            ]
+
+        chunks = [chunk_steps(c) for c in range(S // CHUNK)]
+        n_steps = len(chunks[0])
+        for tick in range(n_steps + LAG * (len(chunks) - 1)):
+            for c, steps in enumerate(chunks):
+                if 0 <= tick - LAG * c < n_steps:
+                    steps[tick - LAG * c]()

@@ -20,6 +20,7 @@ PACK = 4
 CHUNK = 128
 LN_FLOOR = 1e-19
 LEAD = 64
+WEAVES_ON_SCALAR = 3
 LAG = 2
 SQUARES_ON_VECTOR = 2
 
@@ -150,7 +151,7 @@ def tile_picked_yarchi_pay_p_kernel(tc, x_words, x_scales, w1, w2, aa, cap, unit
             g = work.tile([P, PACK, CHUNK], F32, name="g")
             rp = work.tile([P, PACK, CHUNK], F32, name="rp")
             sw = work.tile([P, PACK, CHUNK], F32, name="sw")
-            room = work.tile([P, PACK, CHUNK], F32, name="room")
+            planes = work.tile([P, PACK, CHUNK], BF16, name="planes")
             hid = work.tile([P, CHUNK, PACK], BF16, name="hid", align_bytes=64)
             hid_codes = work.tile([P, CHUNK], U32, name="hid_codes", align_bytes=64)
             hid_scales = work.tile([P, CHUNK], U8, name="hid_scales", align_bytes=64)
@@ -162,6 +163,12 @@ def tile_picked_yarchi_pay_p_kernel(tc, x_words, x_scales, w1, w2, aa, cap, unit
                     nc.vector.tensor_tensor(rc[:], rc[:], rc[:], ALU.mult)
                 else:
                     nc.scalar.activation(rc[:], rc[:], ACT.Square)
+
+            def weave():
+                if c < WEAVES_ON_SCALAR:
+                    nc.scalar.copy(hid[:], planes[:].rearrange("p t j -> p j t"))
+                else:
+                    nc.vector.tensor_copy(hid[:], planes[:].rearrange("p t j -> p j t"))
 
             def last_product():
                 for b in range(N // P):
@@ -181,15 +188,10 @@ def tile_picked_yarchi_pay_p_kernel(tc, x_words, x_scales, w1, w2, aa, cap, unit
                 lambda: nc.vector.scalar_tensor_tensor(g[:], rc[:], 0.2, soft[:], ALU.add, ALU.add),
                 lambda: nc.scalar.activation(rp[:], g[:], ACT.Square, bias=25.0),
                 lambda: nc.scalar.activation(rp[:], rp[:], ACT.Abs_reciprocal_sqrt, scale=50.0, bias=-31250.0),
-                lambda: nc.vector.tensor_scalar(room[:], cap_sb[:, :, cols], -1.0, None, ALU.add),
                 lambda: nc.vector.scalar_tensor_tensor(sw[:], g[:], 50.0, rp[:], ALU.add, ALU.mult),
-                lambda: nc.vector.scalar_tensor_tensor(sw[:], sw[:], -1.0, room[:], ALU.add, ALU.min),
-                lambda: nc.vector.tensor_tensor(
-                    hid[:].rearrange("p (c i) t -> p c t i", i=4),
-                    sw[:].rearrange("p t (c i) -> p c t i", i=4),
-                    outer[:, :, cols].rearrange("p t (c i) -> p c t i", i=4),
-                    ALU.mult,
-                ),
+                lambda: nc.vector.tensor_tensor(sw[:], sw[:], cap_sb[:, :, cols], ALU.min),
+                lambda: nc.vector.scalar_tensor_tensor(planes[:], sw[:], -1.0, outer[:, :, cols], ALU.add, ALU.mult),
+                weave,
                 lambda: nc.vector.quantize_mx(hid_codes[:].bitcast(FP8X4), hid_scales[:], hid[:].rearrange("p j t -> p (j t)")),
                 last_product,
                 lambda: nc.scalar.copy(res[:], acc[:]),

@@ -17,7 +17,7 @@ ACT = mybir.ActivationFunctionType
 
 P = 128
 PACK = 4
-CHUNK = 128
+CHUNKS = (128, 128, 128, 64, 64)
 LN_FLOOR = 1e-19
 LEAD = 64
 WEAVES_ON_SCALAR = 3
@@ -29,7 +29,7 @@ def tile_picked_yarchi_pay_p_kernel(tc, x_words, x_scales, w1, w2, aa, cap, unit
     nc = tc.nc
     with ExitStack() as ctx:
         keep = ctx.enter_context(tc.tile_pool(name="keep", bufs=1))
-        work = ctx.enter_context(tc.tile_pool(name="work", bufs=4))
+        work = ctx.enter_context(tc.tile_pool(name="work", bufs=len(CHUNKS)))
         psum = ctx.enter_context(tc.psum_pool(name="psum", bufs=1))
 
         offs_sb = keep.tile([P, S // 16], U16, name="offs_sb")
@@ -37,22 +37,15 @@ def tile_picked_yarchi_pay_p_kernel(tc, x_words, x_scales, w1, w2, aa, cap, unit
         xw = keep.tile([P, T], U32, name="xw", align_bytes=64)
         xs = keep.tile([P, T], U8, name="xs", align_bytes=64)
         nc.vector.memset(xs[:].bitcast(I32), 0)
+        nc.sync.dma_start(xw[:].bitcast(I32), x_words[0].rearrange("p n r -> p (n r)").bitcast(I32))
         nc.sync.dma_start(offs_sb[:], offs)
         for quad in range(4):
             nc.sync.dma_start(xs[32 * quad : 32 * quad + 4, :].bitcast(I32), x_scales[0, 4 * quad : 4 * quad + 4, :].bitcast(I32))
-        nc.sync.dma_start(xw[:].bitcast(I32), x_words[0].rearrange("p n r -> p (n r)").bitcast(I32))
 
-        def load_halves(w, name):
-            rows = w.rearrange("(p j) c -> p j c", j=PACK)
-            halves = []
-            for h in range(2):
-                raw = keep.tile([P, PACK, H // 2], F32, name=name + str(h))
-                nc.sync.dma_start(raw[:], rows[:, :, h * (H // 2) : (h + 1) * (H // 2)])
-                halves.append(raw)
-            return halves
-
-        w2_raw = load_halves(w2, "w2_raw")
-        w1_raw = load_halves(w1, "w1_raw")
+        w2_raw = keep.tile([P, PACK, H], F32, name="w2_raw")
+        nc.sync.dma_start(w2_raw[:], w2.rearrange("(p j) c -> p j c", j=PACK))
+        w1_raw = keep.tile([P, PACK, H], F32, name="w1_raw")
+        nc.sync.dma_start(w1_raw[:], w1.rearrange("(p j) c -> p j c", j=PACK))
         nc.sync.dma_start(shl_sb[:], shl)
         unit_sb = keep.tile([P, PACK], F32, name="unit_sb")
         nc.sync.dma_start(unit_sb[:], unit.rearrange("(p t) o -> p (t o)", t=PACK))
@@ -65,30 +58,31 @@ def tile_picked_yarchi_pay_p_kernel(tc, x_words, x_scales, w1, w2, aa, cap, unit
 
         x_bytes = keep.tile([P, S], U8, name="x_bytes", align_bytes=64)
         x_codes = keep.tile([P, S], U32, name="x_codes", align_bytes=64)
-        nc.vector.tensor_copy(x_bytes[:], xs[:].indirect(offs_sb[:]))
         nc.vector.tensor_copy(x_codes[:], xw[:].indirect(offs_sb[:]))
+        nc.vector.tensor_copy(x_bytes[:], xs[:].indirect(offs_sb[:]))
 
-        def first_product(raw, name):
-            grouped = keep.tile([P, PACK, P, PACK], BF16, name=name + "_grouped", align_bytes=64)
-            for h in range(2):
-                nc.vector.tensor_copy(
-                    grouped[:, :, h * 64 : (h + 1) * 64, :].rearrange("p t m j -> p m t j"),
-                    raw[h][:].rearrange("p j (m t) -> p m t j", t=PACK),
-                )
+        def first_product(raw, name, staging):
             banks = []
-            for t in range(PACK):
-                codes = keep.tile([P, P], U32, name=name + "_codes" + str(t), align_bytes=64)
-                scales = keep.tile([P, P], U8, name=name + "_scales" + str(t), align_bytes=64)
-                nc.vector.quantize_mx(codes[:].bitcast(FP8X4), scales[:], grouped[:, t].rearrange("p m j -> p (m j)"))
-                bank = psum.tile([P, S], F32, name=name + str(t), tag=name + str(t))
-                nc.tensor.matmul_mx(
-                    bank[:], lhsT=codes[:].bitcast(FP8X4), lhsT_scale=scales[:],
-                    rhs=x_codes[:].bitcast(FP8X4), rhs_scale=x_bytes[:], start=True, stop=True,
+            for pair in range(PACK // 2):
+                grouped = keep.tile([P, 2, P, PACK], BF16, name=staging[pair], align_bytes=64)
+                nc.vector.tensor_copy(
+                    grouped[:].rearrange("p t m j -> p m j t"),
+                    raw[:].rearrange("p j (m t) -> p m j t", t=PACK)[:, :, :, 2 * pair : 2 * pair + 2],
                 )
-                banks.append(bank)
+                for half in range(2):
+                    t = 2 * pair + half
+                    codes = keep.tile([P, P], U32, name=name + "_codes" + str(t), align_bytes=64)
+                    scales = keep.tile([P, P], U8, name=name + "_scales" + str(t), align_bytes=64)
+                    nc.vector.quantize_mx(codes[:].bitcast(FP8X4), scales[:], grouped[:, half].rearrange("p m j -> p (m j)"))
+                    bank = psum.tile([P, S], F32, name=name + str(t), tag=name + str(t))
+                    nc.tensor.matmul_mx(
+                        bank[:], lhsT=codes[:].bitcast(FP8X4), lhsT_scale=scales[:],
+                        rhs=x_codes[:].bitcast(FP8X4), rhs_scale=x_bytes[:], start=True, stop=True,
+                    )
+                    banks.append(bank)
             return banks
 
-        rt_banks = first_product(w2_raw, "rt")
+        rt_banks = first_product(w2_raw, "rt", ("w2_grouped", "w2_grouped"))
         sg = keep.tile([P, PACK, S], F32, name="sg")
         nc.scalar.activation(sg[:, 0, :LEAD], rt_banks[0][:, :LEAD], ACT.Sigmoid, scale=-1.0)
         windows = []
@@ -97,7 +91,7 @@ def tile_picked_yarchi_pay_p_kernel(tc, x_words, x_scales, w1, w2, aa, cap, unit
             nc.scalar.copy(window[:], rt_banks[t][:])
             windows.append(window)
 
-        po_banks = first_product(w1_raw, "po")
+        po_banks = first_product(w1_raw, "po", ("w1_grouped0", "w1_grouped1"))
 
         rt = keep.tile([P, PACK, S], F32, name="rt_sb")
         diff = keep.tile([P, PACK, S], F32, name="diff")
@@ -110,10 +104,10 @@ def tile_picked_yarchi_pay_p_kernel(tc, x_words, x_scales, w1, w2, aa, cap, unit
         sig = keep.tile([P, PACK, S], F32, name="sig")
         sand = keep.tile([P, PACK, S], F32, name="sand")
         for t in range(PACK):
-            nc.scalar.activation(sig[:, t, :], po_banks[t][:], ACT.Sigmoid)
-        for t in range(PACK):
             first = LEAD if t == 0 else 0
             nc.scalar.activation(sg[:, t, first:], rt_banks[t][:, first:], ACT.Sigmoid, scale=-1.0)
+        for t in range(PACK):
+            nc.scalar.activation(sig[:, t, :], po_banks[t][:], ACT.Sigmoid)
         for t in range(PACK):
             nc.scalar.activation(sand[:, t, :], diff[:, t, :], ACT.Sigmoid, scale=-1.0)
 
@@ -142,21 +136,22 @@ def tile_picked_yarchi_pay_p_kernel(tc, x_words, x_scales, w1, w2, aa, cap, unit
         out_rows = out.rearrange("(b m) j -> m b j", m=P)
 
         def chunk_steps(c):
-            cols = slice(c * CHUNK, (c + 1) * CHUNK)
-            soft = work.tile([P, PACK, CHUNK], F32, name="soft")
-            x0 = work.tile([P, PACK, CHUNK], F32, name="x0")
-            x1 = work.tile([P, PACK, CHUNK], F32, name="x1")
-            x2 = work.tile([P, PACK, CHUNK], F32, name="x2")
-            rc = work.tile([P, PACK, CHUNK], F32, name="rc")
-            g = work.tile([P, PACK, CHUNK], F32, name="g")
-            rp = work.tile([P, PACK, CHUNK], F32, name="rp")
-            sw = work.tile([P, PACK, CHUNK], F32, name="sw")
-            planes = work.tile([P, PACK, CHUNK], BF16, name="planes")
-            hid = work.tile([P, CHUNK, PACK], BF16, name="hid", align_bytes=64)
-            hid_codes = work.tile([P, CHUNK], U32, name="hid_codes", align_bytes=64)
-            hid_scales = work.tile([P, CHUNK], U8, name="hid_scales", align_bytes=64)
-            acc = psum.tile([P, N // P, CHUNK], F32, name="acc", tag="po" + str(c))
-            res = work.tile([P, N // P, CHUNK], F32, name="res")
+            width = CHUNKS[c]
+            cols = slice(sum(CHUNKS[:c]), sum(CHUNKS[: c + 1]))
+            soft = work.tile([P, PACK, width], F32, name="soft")
+            x0 = work.tile([P, PACK, width], F32, name="x0")
+            x1 = work.tile([P, PACK, width], F32, name="x1")
+            x2 = work.tile([P, PACK, width], F32, name="x2")
+            rc = work.tile([P, PACK, width], F32, name="rc")
+            g = work.tile([P, PACK, width], F32, name="g")
+            rp = work.tile([P, PACK, width], F32, name="rp")
+            sw = work.tile([P, PACK, width], F32, name="sw")
+            planes = work.tile([P, PACK, width], BF16, name="planes")
+            hid = work.tile([P, width, PACK], BF16, name="hid", align_bytes=64)
+            hid_codes = work.tile([P, width], U32, name="hid_codes", align_bytes=64)
+            hid_scales = work.tile([P, width], U8, name="hid_scales", align_bytes=64)
+            acc = psum.tile([P, N // P, width], F32, name="acc", tag=("po0", "po1", "po2", "po3", "rt0")[c])
+            res = work.tile([P, N // P, width], F32, name="res")
 
             def square_rc():
                 if c < SQUARES_ON_VECTOR:
@@ -198,7 +193,7 @@ def tile_picked_yarchi_pay_p_kernel(tc, x_words, x_scales, w1, w2, aa, cap, unit
                 lambda: nc.sync.dma_start(out_rows[:, :, cols], res[:]),
             ]
 
-        chunks = [chunk_steps(c) for c in range(S // CHUNK)]
+        chunks = [chunk_steps(c) for c in range(len(CHUNKS))]
         n_steps = len(chunks[0])
         for tick in range(n_steps + LAG * (len(chunks) - 1)):
             for c, steps in enumerate(chunks):

@@ -17,12 +17,17 @@ ACT = mybir.ActivationFunctionType
 
 P = 128
 PACK = 4
-CHUNKS = (128, 128, 128, 64, 64)
+LIST_ROWS = 16
+PLANE_BYTES = S * 4
+GATHER = 256
+
 LN_FLOOR = 1e-19
 LEAD = 64
-WEAVES_ON_SCALAR = 3
+CHUNKS = (128, 128, 128, 64, 64)
 LAG = 2
+COPIES_ON_VECTOR = 2
 SQUARES_ON_VECTOR = 2
+WEAVES_ON_SCALAR = 3
 
 
 def tile_picked_yarchi_pay_p_kernel(tc, x_words, x_scales, w1, w2, aa, cap, unit, w3, offs, shl, out):
@@ -30,18 +35,18 @@ def tile_picked_yarchi_pay_p_kernel(tc, x_words, x_scales, w1, w2, aa, cap, unit
     with ExitStack() as ctx:
         keep = ctx.enter_context(tc.tile_pool(name="keep", bufs=1))
         work = ctx.enter_context(tc.tile_pool(name="work", bufs=len(CHUNKS)))
+        shared = ctx.enter_context(tc.tile_pool(name="shared", bufs=1))
         psum = ctx.enter_context(tc.psum_pool(name="psum", bufs=1))
 
-        offs_sb = keep.tile([P, S // 16], U16, name="offs_sb")
-        shl_sb = keep.tile([P, S // 16], U16, name="shl_sb")
-        xw = keep.tile([P, T], U32, name="xw", align_bytes=64)
-        xs = keep.tile([P, T], U8, name="xs", align_bytes=64)
-        nc.vector.memset(xs[:].bitcast(I32), 0)
-        nc.sync.dma_start(xw[:].bitcast(I32), x_words[0].rearrange("p n r -> p (n r)").bitcast(I32))
+        offs_sb = keep.tile([P, S // LIST_ROWS], U16, name="offs_sb")
+        shl_sb = keep.tile([P, S // LIST_ROWS], U16, name="shl_sb")
+        table_words = keep.tile([P, T], U32, name="table_words", align_bytes=64)
+        table_bytes = keep.tile([P, T], U8, name="table_bytes", align_bytes=64)
+        nc.vector.memset(table_bytes[:].bitcast(I32), 0)
+        nc.sync.dma_start(table_words[:].bitcast(I32), x_words[0].rearrange("p n r -> p (n r)").bitcast(I32))
         nc.sync.dma_start(offs_sb[:], offs)
         for quad in range(4):
-            nc.sync.dma_start(xs[32 * quad : 32 * quad + 4, :].bitcast(I32), x_scales[0, 4 * quad : 4 * quad + 4, :].bitcast(I32))
-
+            nc.sync.dma_start(table_bytes[32 * quad : 32 * quad + 4, :].bitcast(I32), x_scales[0, 4 * quad : 4 * quad + 4, :].bitcast(I32))
         w2_raw = keep.tile([P, PACK, H], F32, name="w2_raw")
         nc.sync.dma_start(w2_raw[:], w2.rearrange("(p j) c -> p j c", j=PACK))
         w1_raw = keep.tile([P, PACK, H], F32, name="w1_raw")
@@ -49,24 +54,18 @@ def tile_picked_yarchi_pay_p_kernel(tc, x_words, x_scales, w1, w2, aa, cap, unit
         nc.sync.dma_start(shl_sb[:], shl)
         unit_sb = keep.tile([P, PACK], F32, name="unit_sb")
         nc.sync.dma_start(unit_sb[:], unit.rearrange("(p t) o -> p (t o)", t=PACK))
-        aa_sb = keep.tile([P, PACK, S], F32, name="aa_sb")
-        nc.sync.dma_start(aa_sb[:], aa.rearrange("(p t) j -> p t j", t=PACK))
-        cap_sb = keep.tile([P, PACK, S], F32, name="cap_sb")
-        nc.sync.dma_start(cap_sb[:], cap.rearrange("(p t) j -> p t j", t=PACK))
-        w3_raw = keep.tile([P, PACK, N], F32, name="w3_raw")
-        nc.sync.dma_start(w3_raw[:], w3.rearrange("(p t) m -> p t m", t=PACK))
 
         x_bytes = keep.tile([P, S], U8, name="x_bytes", align_bytes=64)
         x_codes = keep.tile([P, S], U32, name="x_codes", align_bytes=64)
-        nc.vector.tensor_copy(x_codes[:], xw[:].indirect(offs_sb[:]))
-        nc.vector.tensor_copy(x_bytes[:], xs[:].indirect(offs_sb[:]))
+        nc.vector.tensor_copy(x_codes[:], table_words[:].indirect(offs_sb[:]))
+        nc.vector.tensor_copy(x_bytes[:], table_bytes[:].indirect(offs_sb[:]))
 
         def first_product(raw, name, staging):
             banks = []
             for pair in range(PACK // 2):
                 grouped = keep.tile([P, 2, P, PACK], BF16, name=staging[pair], align_bytes=64)
                 nc.vector.tensor_copy(
-                    grouped[:].rearrange("p t m j -> p m j t"),
+                    grouped[:].rearrange("p h m j -> p m j h"),
                     raw[:].rearrange("p j (m t) -> p m j t", t=PACK)[:, :, :, 2 * pair : 2 * pair + 2],
                 )
                 for half in range(2):
@@ -83,46 +82,59 @@ def tile_picked_yarchi_pay_p_kernel(tc, x_words, x_scales, w1, w2, aa, cap, unit
             return banks
 
         rt_banks = first_product(w2_raw, "rt", ("w2_grouped", "w2_grouped"))
-        sg = keep.tile([P, PACK, S], F32, name="sg")
-        nc.scalar.activation(sg[:, 0, :LEAD], rt_banks[0][:, :LEAD], ACT.Sigmoid, scale=-1.0)
+        sig_neg_rt = keep.tile([P, PACK, S], F32, name="sig_neg_rt")
+        nc.scalar.activation(sig_neg_rt[:, 0, :LEAD], rt_banks[0][:, :LEAD], ACT.Sigmoid, scale=-1.0)
         windows = []
         for t in range(PACK):
-            window = keep.tile([P, S], F32, name="window" + str(t))
+            window = shared.tile([P, S], F32, name="window" + str(t), offset=t * PACK * PLANE_BYTES)
             nc.scalar.copy(window[:], rt_banks[t][:])
             windows.append(window)
 
         po_banks = first_product(w1_raw, "po", ("w1_grouped0", "w1_grouped1"))
 
-        rt = keep.tile([P, PACK, S], F32, name="rt_sb")
-        diff = keep.tile([P, PACK, S], F32, name="diff")
+        rt = [keep.tile([P, S], F32, name="rt_sb" + str(t)) for t in range(PACK)]
+        rs_less_rt = keep.tile([P, PACK, S], F32, name="rs_less_rt")
         for t in range(PACK):
-            nc.vector.tensor_copy(rt[:, t, :], windows[t][:])
-            for h in range(2):
-                cols = slice(h * 256, (h + 1) * 256)
-                nc.vector.tensor_tensor(diff[:, t, cols], windows[t][:].indirect(shl_sb[:, h * 16 : (h + 1) * 16]), rt[:, t, cols], ALU.subtract)
+            if t < COPIES_ON_VECTOR:
+                nc.vector.tensor_copy(rt[t][:], windows[t][:])
+            else:
+                nc.sync.dma_start(rt[t][:], windows[t][:])
+            for first in range(0, S, GATHER):
+                cols = slice(first, first + GATHER)
+                offsets = shl_sb[:, first // LIST_ROWS : (first + GATHER) // LIST_ROWS]
+                nc.vector.tensor_tensor(rs_less_rt[:, t, cols], windows[t][:].indirect(offsets), rt[t][:, cols], ALU.subtract)
 
-        sig = keep.tile([P, PACK, S], F32, name="sig")
+        aa_sb = shared.tile([P, PACK, S], F32, name="aa_sb", offset=0)
+        nc.sync.dma_start(aa_sb[:], aa.rearrange("(p t) j -> p t j", t=PACK))
+        cap_sb = shared.tile([P, PACK, S], F32, name="cap_sb", offset=PACK * PLANE_BYTES)
+        nc.sync.dma_start(cap_sb[:], cap.rearrange("(p t) j -> p t j", t=PACK))
+        w3_raw = shared.tile([P, PACK, N], F32, name="w3_raw", offset=2 * PACK * PLANE_BYTES)
+        nc.sync.dma_start(w3_raw[:], w3.rearrange("(p t) m -> p t m", t=PACK))
+
+        sig_po = keep.tile([P, PACK, S], F32, name="sig_po")
         sand = keep.tile([P, PACK, S], F32, name="sand")
         for t in range(PACK):
-            first = LEAD if t == 0 else 0
-            nc.scalar.activation(sg[:, t, first:], rt_banks[t][:, first:], ACT.Sigmoid, scale=-1.0)
+            done = LEAD if t == 0 else 0
+            nc.scalar.activation(sig_neg_rt[:, t, done:], rt_banks[t][:, done:], ACT.Sigmoid, scale=-1.0)
         for t in range(PACK):
-            nc.scalar.activation(sig[:, t, :], po_banks[t][:], ACT.Sigmoid)
+            nc.scalar.activation(sig_po[:, t, :], po_banks[t][:], ACT.Sigmoid)
         for t in range(PACK):
-            nc.scalar.activation(sand[:, t, :], diff[:, t, :], ACT.Sigmoid, scale=-1.0)
+            nc.scalar.activation(sand[:, t, :], rs_less_rt[:, t, :], ACT.Sigmoid, scale=-1.0)
 
-        nc.scalar.activation(diff[:], sg[:], ACT.Ln, bias=LN_FLOOR)
+        ln_sig = rs_less_rt
+        rsqrt_aa = sig_neg_rt
+        nc.scalar.activation(ln_sig[:], sig_neg_rt[:], ACT.Ln, bias=LN_FLOOR)
 
         gain = keep.tile([P, PACK], F32, name="gain")
         nc.vector.tensor_scalar(gain[:], unit_sb[:], -0.4, None, ALU.mult)
         outer = keep.tile([P, PACK, S], F32, name="outer")
-        zs = []
+        por_sand = []
         for t in range(PACK):
-            z = work.tile([P, S], F32, name="z")
-            nc.vector.scalar_tensor_tensor(z[:], sig[:, t, :], 0.125, sand[:, t, :], ALU.add, ALU.mult)
-            zs.append(z)
+            plane = work.tile([P, S], F32, name="por_sand")
+            nc.vector.scalar_tensor_tensor(plane[:], sig_po[:, t, :], 0.125, sand[:, t, :], ALU.add, ALU.mult)
+            por_sand.append(plane)
         for t in range(PACK):
-            nc.vector.scalar_tensor_tensor(outer[:, t, :], zs[t][:], gain[:, t : t + 1], sand[:, t, :], ALU.mult, ALU.mult)
+            nc.vector.scalar_tensor_tensor(outer[:, t, :], por_sand[t][:], gain[:, t : t + 1], sand[:, t, :], ALU.mult, ALU.mult)
 
         w3_grouped = keep.tile([P, N, PACK], BF16, name="w3_grouped", align_bytes=64)
         nc.vector.tensor_copy(
@@ -133,37 +145,41 @@ def tile_picked_yarchi_pay_p_kernel(tc, x_words, x_scales, w1, w2, aa, cap, unit
         w3_scales = keep.tile([P, N], U8, name="w3_scales", align_bytes=64)
         nc.vector.quantize_mx(w3_codes[:].bitcast(FP8X4), w3_scales[:], w3_grouped[:].rearrange("p m t -> p (m t)"))
 
+        softplus = keep.tile([P, PACK, S], F32, name="softplus")
+        for t in range(PACK):
+            nc.vector.scalar_tensor_tensor(softplus[:, t, :], ln_sig[:, t, :], -1.0, rt[t][:], ALU.mult, ALU.max)
+
         out_rows = out.rearrange("(b m) j -> m b j", m=P)
+        free_banks = ("po0", "po1", "po2", "po3", "rt0")
 
         def chunk_steps(c):
             width = CHUNKS[c]
             cols = slice(sum(CHUNKS[:c]), sum(CHUNKS[: c + 1]))
-            soft = work.tile([P, PACK, width], F32, name="soft")
-            x0 = work.tile([P, PACK, width], F32, name="x0")
-            x1 = work.tile([P, PACK, width], F32, name="x1")
-            x2 = work.tile([P, PACK, width], F32, name="x2")
-            rc = work.tile([P, PACK, width], F32, name="rc")
+            root_ff = work.tile([P, PACK, width], F32, name="root_ff")
+            inv_ff = work.tile([P, PACK, width], F32, name="inv_ff")
+            cond_less_half = work.tile([P, PACK, width], F32, name="cond_less_half")
+            inv_cond = work.tile([P, PACK, width], F32, name="inv_cond")
             g = work.tile([P, PACK, width], F32, name="g")
-            rp = work.tile([P, PACK, width], F32, name="rp")
+            root = work.tile([P, PACK, width], F32, name="root")
             sw = work.tile([P, PACK, width], F32, name="sw")
-            planes = work.tile([P, PACK, width], BF16, name="planes")
+            hid_planes = work.tile([P, PACK, width], BF16, name="hid_planes")
             hid = work.tile([P, width, PACK], BF16, name="hid", align_bytes=64)
             hid_codes = work.tile([P, width], U32, name="hid_codes", align_bytes=64)
             hid_scales = work.tile([P, width], U8, name="hid_scales", align_bytes=64)
-            acc = psum.tile([P, N // P, width], F32, name="acc", tag=("po0", "po1", "po2", "po3", "rt0")[c])
-            res = work.tile([P, N // P, width], F32, name="res")
+            acc = psum.tile([P, N // P, width], F32, name="acc", tag=free_banks[c])
+            result = work.tile([P, N // P, width], F32, name="result")
 
-            def square_rc():
+            def square_inv_cond():
                 if c < SQUARES_ON_VECTOR:
-                    nc.vector.tensor_tensor(rc[:], rc[:], rc[:], ALU.mult)
+                    nc.vector.tensor_tensor(inv_cond[:], inv_cond[:], inv_cond[:], ALU.mult)
                 else:
-                    nc.scalar.activation(rc[:], rc[:], ACT.Square)
+                    nc.scalar.activation(inv_cond[:], inv_cond[:], ACT.Square)
 
             def weave():
                 if c < WEAVES_ON_SCALAR:
-                    nc.scalar.copy(hid[:], planes[:].rearrange("p t j -> p j t"))
+                    nc.scalar.copy(hid[:], hid_planes[:].rearrange("p t j -> p j t"))
                 else:
-                    nc.vector.tensor_copy(hid[:], planes[:].rearrange("p t j -> p j t"))
+                    nc.vector.tensor_copy(hid[:], hid_planes[:].rearrange("p t j -> p j t"))
 
             def last_product():
                 for b in range(N // P):
@@ -173,24 +189,23 @@ def tile_picked_yarchi_pay_p_kernel(tc, x_words, x_scales, w1, w2, aa, cap, unit
                     )
 
             return [
-                lambda: nc.scalar.activation(sg[:, :, cols], aa_sb[:, :, cols], ACT.Abs_reciprocal_sqrt),
-                lambda: nc.vector.scalar_tensor_tensor(x0[:], sig[:, :, cols], 0.125, sg[:, :, cols], ALU.add, ALU.mult),
-                lambda: nc.scalar.activation(x1[:], x0[:], ACT.Square, scale=0.4),
-                lambda: nc.vector.scalar_tensor_tensor(x2[:], x1[:], -0.5, sand[:, :, cols], ALU.add, ALU.mult),
-                lambda: nc.scalar.activation(rc[:], x2[:], ACT.Abs_reciprocal_sqrt, scale=10.0, bias=5.0),
-                square_rc,
-                lambda: nc.vector.scalar_tensor_tensor(soft[:], diff[:, :, cols], -1.0, rt[:, :, cols], ALU.mult, ALU.max),
-                lambda: nc.vector.scalar_tensor_tensor(g[:], rc[:], 0.2, soft[:], ALU.add, ALU.add),
-                lambda: nc.scalar.activation(rp[:], g[:], ACT.Square, bias=25.0),
-                lambda: nc.scalar.activation(rp[:], rp[:], ACT.Abs_reciprocal_sqrt, scale=50.0, bias=-31250.0),
-                lambda: nc.vector.scalar_tensor_tensor(sw[:], g[:], 50.0, rp[:], ALU.add, ALU.mult),
+                lambda: nc.scalar.activation(rsqrt_aa[:, :, cols], aa_sb[:, :, cols], ACT.Abs_reciprocal_sqrt),
+                lambda: nc.vector.scalar_tensor_tensor(root_ff[:], sig_po[:, :, cols], 0.125, rsqrt_aa[:, :, cols], ALU.add, ALU.mult),
+                lambda: nc.scalar.activation(inv_ff[:], root_ff[:], ACT.Square, scale=0.4),
+                lambda: nc.vector.scalar_tensor_tensor(cond_less_half[:], inv_ff[:], -0.5, sand[:, :, cols], ALU.add, ALU.mult),
+                lambda: nc.scalar.activation(inv_cond[:], cond_less_half[:], ACT.Abs_reciprocal_sqrt, scale=10.0, bias=5.0),
+                square_inv_cond,
+                lambda: nc.vector.scalar_tensor_tensor(g[:], inv_cond[:], 0.2, softplus[:, :, cols], ALU.add, ALU.add),
+                lambda: nc.scalar.activation(root[:], g[:], ACT.Square, bias=25.0),
+                lambda: nc.scalar.activation(root[:], root[:], ACT.Abs_reciprocal_sqrt, scale=50.0, bias=-50.0 * 625.0),
+                lambda: nc.vector.scalar_tensor_tensor(sw[:], g[:], 50.0, root[:], ALU.add, ALU.mult),
                 lambda: nc.vector.tensor_tensor(sw[:], sw[:], cap_sb[:, :, cols], ALU.min),
-                lambda: nc.vector.scalar_tensor_tensor(planes[:], sw[:], -1.0, outer[:, :, cols], ALU.add, ALU.mult),
+                lambda: nc.vector.scalar_tensor_tensor(hid_planes[:], sw[:], -1.0, outer[:, :, cols], ALU.add, ALU.mult),
                 weave,
                 lambda: nc.vector.quantize_mx(hid_codes[:].bitcast(FP8X4), hid_scales[:], hid[:].rearrange("p j t -> p (j t)")),
                 last_product,
-                lambda: nc.scalar.copy(res[:], acc[:]),
-                lambda: nc.sync.dma_start(out_rows[:, :, cols], res[:]),
+                lambda: nc.scalar.copy(result[:], acc[:]),
+                lambda: nc.sync.dma_start(out_rows[:, :, cols], result[:]),
             ]
 
         chunks = [chunk_steps(c) for c in range(len(CHUNKS))]

from contextlib import ExitStack

import concourse.mybir as mybir

K, T, S, N, H = 512, 1024, 512, 256, 512
FLOPS = 2 * K * H * S * 2 + 2 * H * N * S

F32 = mybir.dt.float32
BF16 = mybir.dt.bfloat16
I32 = mybir.dt.int32
U32 = mybir.dt.uint32
U16 = mybir.dt.uint16
U8 = mybir.dt.uint8
FP8X4 = mybir.dt.float8_e4m3fn_x4
ALU = mybir.AluOpType
ACT = mybir.ActivationFunctionType

P = 128
PACK = 4
LIST_ROWS = 16
PLANE_BYTES = S * 4
GATHER = 256

LN_FLOOR = 1e-19
LEAD = 64
CHUNKS = (128, 128, 128, 64, 64)
LAG = 2
COPIES_ON_VECTOR = 2
SQUARES_ON_VECTOR = 2
WEAVES_ON_SCALAR = 3


def tile_picked_yarchi_pay_p_kernel(tc, x_words, x_scales, w1, w2, aa, cap, unit, w3, offs, shl, out):
    nc = tc.nc
    with ExitStack() as ctx:
        keep = ctx.enter_context(tc.tile_pool(name="keep", bufs=1))
        work = ctx.enter_context(tc.tile_pool(name="work", bufs=len(CHUNKS)))
        shared = ctx.enter_context(tc.tile_pool(name="shared", bufs=1))
        psum = ctx.enter_context(tc.psum_pool(name="psum", bufs=1))

        offs_sb = keep.tile([P, S // LIST_ROWS], U16, name="offs_sb")
        shl_sb = keep.tile([P, S // LIST_ROWS], U16, name="shl_sb")
        table_words = keep.tile([P, T], U32, name="table_words", align_bytes=64)
        table_bytes = keep.tile([P, T], U8, name="table_bytes", align_bytes=64)
        nc.vector.memset(table_bytes[:].bitcast(I32), 0)
        nc.sync.dma_start(table_words[:].bitcast(I32), x_words[0].rearrange("p n r -> p (n r)").bitcast(I32))
        nc.sync.dma_start(offs_sb[:], offs)
        for quad in range(4):
            nc.sync.dma_start(table_bytes[32 * quad : 32 * quad + 4, :].bitcast(I32), x_scales[0, 4 * quad : 4 * quad + 4, :].bitcast(I32))
        w2_raw = keep.tile([P, PACK, H], F32, name="w2_raw")
        nc.sync.dma_start(w2_raw[:], w2.rearrange("(p j) c -> p j c", j=PACK))
        w1_raw = keep.tile([P, PACK, H], F32, name="w1_raw")
        nc.sync.dma_start(w1_raw[:], w1.rearrange("(p j) c -> p j c", j=PACK))
        nc.sync.dma_start(shl_sb[:], shl)
        unit_sb = keep.tile([P, PACK], F32, name="unit_sb")
        nc.sync.dma_start(unit_sb[:], unit.rearrange("(p t) o -> p (t o)", t=PACK))

        x_bytes = keep.tile([P, S], U8, name="x_bytes", align_bytes=64)
        x_codes = keep.tile([P, S], U32, name="x_codes", align_bytes=64)
        nc.vector.tensor_copy(x_codes[:], table_words[:].indirect(offs_sb[:]))
        nc.vector.tensor_copy(x_bytes[:], table_bytes[:].indirect(offs_sb[:]))

        def first_product(raw, name, staging):
            banks = []
            for pair in range(PACK // 2):
                grouped = keep.tile([P, 2, P, PACK], BF16, name=staging[pair], align_bytes=64)
                nc.vector.tensor_copy(
                    grouped[:].rearrange("p h m j -> p m j h"),
                    raw[:].rearrange("p j (m t) -> p m j t", t=PACK)[:, :, :, 2 * pair : 2 * pair + 2],
                )
                for half in range(2):
                    t = 2 * pair + half
                    codes = keep.tile([P, P], U32, name=name + "_codes" + str(t), align_bytes=64)
                    scales = keep.tile([P, P], U8, name=name + "_scales" + str(t), align_bytes=64)
                    nc.vector.quantize_mx(codes[:].bitcast(FP8X4), scales[:], grouped[:, half].rearrange("p m j -> p (m j)"))
                    bank = psum.tile([P, S], F32, name=name + str(t), tag=name + str(t))
                    nc.tensor.matmul_mx(
                        bank[:], lhsT=codes[:].bitcast(FP8X4), lhsT_scale=scales[:],
                        rhs=x_codes[:].bitcast(FP8X4), rhs_scale=x_bytes[:], start=True, stop=True,
                    )
                    banks.append(bank)
            return banks

        rt_banks = first_product(w2_raw, "rt", ("w2_grouped", "w2_grouped"))
        sig_neg_rt = keep.tile([P, PACK, S], F32, name="sig_neg_rt")
        nc.scalar.activation(sig_neg_rt[:, 0, :LEAD], rt_banks[0][:, :LEAD], ACT.Sigmoid, scale=-1.0)
        windows = []
        for t in range(PACK):
            window = shared.tile([P, S], F32, name="window" + str(t), offset=t * PACK * PLANE_BYTES)
            nc.scalar.copy(window[:], rt_banks[t][:])
            windows.append(window)

        po_banks = first_product(w1_raw, "po", ("w1_grouped0", "w1_grouped1"))

        rt = [keep.tile([P, S], F32, name="rt_sb" + str(t)) for t in range(PACK)]
        rs_less_rt = keep.tile([P, PACK, S], F32, name="rs_less_rt")
        for t in range(PACK):
            if t < COPIES_ON_VECTOR:
                nc.vector.tensor_copy(rt[t][:], windows[t][:])
            else:
                nc.sync.dma_start(rt[t][:], windows[t][:])
            for first in range(0, S, GATHER):
                cols = slice(first, first + GATHER)
                offsets = shl_sb[:, first // LIST_ROWS : (first + GATHER) // LIST_ROWS]
                nc.vector.tensor_tensor(rs_less_rt[:, t, cols], windows[t][:].indirect(offsets), rt[t][:, cols], ALU.subtract)

        aa_sb = shared.tile([P, PACK, S], F32, name="aa_sb", offset=0)
        nc.sync.dma_start(aa_sb[:], aa.rearrange("(p t) j -> p t j", t=PACK))
        cap_sb = shared.tile([P, PACK, S], F32, name="cap_sb", offset=PACK * PLANE_BYTES)
        nc.sync.dma_start(cap_sb[:], cap.rearrange("(p t) j -> p t j", t=PACK))
        w3_raw = shared.tile([P, PACK, N], F32, name="w3_raw", offset=2 * PACK * PLANE_BYTES)
        nc.sync.dma_start(w3_raw[:], w3.rearrange("(p t) m -> p t m", t=PACK))

        sig_po = keep.tile([P, PACK, S], F32, name="sig_po")
        sand = keep.tile([P, PACK, S], F32, name="sand")
        for t in range(PACK):
            done = LEAD if t == 0 else 0
            nc.scalar.activation(sig_neg_rt[:, t, done:], rt_banks[t][:, done:], ACT.Sigmoid, scale=-1.0)
        for t in range(PACK):
            nc.scalar.activation(sig_po[:, t, :], po_banks[t][:], ACT.Sigmoid)
        for t in range(PACK):
            nc.scalar.activation(sand[:, t, :], rs_less_rt[:, t, :], ACT.Sigmoid, scale=-1.0)

        ln_sig = rs_less_rt
        rsqrt_aa = sig_neg_rt
        nc.scalar.activation(ln_sig[:], sig_neg_rt[:], ACT.Ln, bias=LN_FLOOR)

        gain = keep.tile([P, PACK], F32, name="gain")
        nc.vector.tensor_scalar(gain[:], unit_sb[:], -0.4, None, ALU.mult)
        outer = keep.tile([P, PACK, S], F32, name="outer")
        por_sand = []
        for t in range(PACK):
            plane = work.tile([P, S], F32, name="por_sand")
            nc.vector.scalar_tensor_tensor(plane[:], sig_po[:, t, :], 0.125, sand[:, t, :], ALU.add, ALU.mult)
            por_sand.append(plane)
        for t in range(PACK):
            nc.vector.scalar_tensor_tensor(outer[:, t, :], por_sand[t][:], gain[:, t : t + 1], sand[:, t, :], ALU.mult, ALU.mult)

        w3_grouped = keep.tile([P, N, PACK], BF16, name="w3_grouped", align_bytes=64)
        nc.vector.tensor_copy(
            w3_grouped[:].rearrange("p (c i) t -> p c t i", i=4),
            w3_raw[:].rearrange("p t (c i) -> p c t i", i=4),
        )
        w3_codes = keep.tile([P, N], U32, name="w3_codes", align_bytes=64)
        w3_scales = keep.tile([P, N], U8, name="w3_scales", align_bytes=64)
        nc.vector.quantize_mx(w3_codes[:].bitcast(FP8X4), w3_scales[:], w3_grouped[:].rearrange("p m t -> p (m t)"))

        softplus = keep.tile([P, PACK, S], F32, name="softplus")
        for t in range(PACK):
            nc.vector.scalar_tensor_tensor(softplus[:, t, :], ln_sig[:, t, :], -1.0, rt[t][:], ALU.mult, ALU.max)

        out_rows = out.rearrange("(b m) j -> m b j", m=P)
        free_banks = ("po0", "po1", "po2", "po3", "rt0")

        def chunk_steps(c):
            width = CHUNKS[c]
            cols = slice(sum(CHUNKS[:c]), sum(CHUNKS[: c + 1]))
            root_ff = work.tile([P, PACK, width], F32, name="root_ff")
            inv_ff = work.tile([P, PACK, width], F32, name="inv_ff")
            cond_less_half = work.tile([P, PACK, width], F32, name="cond_less_half")
            inv_cond = work.tile([P, PACK, width], F32, name="inv_cond")
            g = work.tile([P, PACK, width], F32, name="g")
            root = work.tile([P, PACK, width], F32, name="root")
            sw = work.tile([P, PACK, width], F32, name="sw")
            hid_planes = work.tile([P, PACK, width], BF16, name="hid_planes")
            hid = work.tile([P, width, PACK], BF16, name="hid", align_bytes=64)
            hid_codes = work.tile([P, width], U32, name="hid_codes", align_bytes=64)
            hid_scales = work.tile([P, width], U8, name="hid_scales", align_bytes=64)
            acc = psum.tile([P, N // P, width], F32, name="acc", tag=free_banks[c])
            result = work.tile([P, N // P, width], F32, name="result")

            def square_inv_cond():
                if c < SQUARES_ON_VECTOR:
                    nc.vector.tensor_tensor(inv_cond[:], inv_cond[:], inv_cond[:], ALU.mult)
                else:
                    nc.scalar.activation(inv_cond[:], inv_cond[:], ACT.Square)

            def weave():
                if c < WEAVES_ON_SCALAR:
                    nc.scalar.copy(hid[:], hid_planes[:].rearrange("p t j -> p j t"))
                else:
                    nc.vector.tensor_copy(hid[:], hid_planes[:].rearrange("p t j -> p j t"))

            def last_product():
                for b in range(N // P):
                    nc.tensor.matmul_mx(
                        acc[:, b, :], lhsT=w3_codes[:, b * P : (b + 1) * P].bitcast(FP8X4), lhsT_scale=w3_scales[:, b * P : (b + 1) * P],
                        rhs=hid_codes[:].bitcast(FP8X4), rhs_scale=hid_scales[:], start=True, stop=True,
                    )

            return [
                lambda: nc.scalar.activation(rsqrt_aa[:, :, cols], aa_sb[:, :, cols], ACT.Abs_reciprocal_sqrt),
                lambda: nc.vector.scalar_tensor_tensor(root_ff[:], sig_po[:, :, cols], 0.125, rsqrt_aa[:, :, cols], ALU.add, ALU.mult),
                lambda: nc.scalar.activation(inv_ff[:], root_ff[:], ACT.Square, scale=0.4),
                lambda: nc.vector.scalar_tensor_tensor(cond_less_half[:], inv_ff[:], -0.5, sand[:, :, cols], ALU.add, ALU.mult),
                lambda: nc.scalar.activation(inv_cond[:], cond_less_half[:], ACT.Abs_reciprocal_sqrt, scale=10.0, bias=5.0),
                square_inv_cond,
                lambda: nc.vector.scalar_tensor_tensor(g[:], inv_cond[:], 0.2, softplus[:, :, cols], ALU.add, ALU.add),
                lambda: nc.scalar.activation(root[:], g[:], ACT.Square, bias=25.0),
                lambda: nc.scalar.activation(root[:], root[:], ACT.Abs_reciprocal_sqrt, scale=50.0, bias=-50.0 * 625.0),
                lambda: nc.vector.scalar_tensor_tensor(sw[:], g[:], 50.0, root[:], ALU.add, ALU.mult),
                lambda: nc.vector.tensor_tensor(sw[:], sw[:], cap_sb[:, :, cols], ALU.min),
                lambda: nc.vector.scalar_tensor_tensor(hid_planes[:], sw[:], -1.0, outer[:, :, cols], ALU.add, ALU.mult),
                weave,
                lambda: nc.vector.quantize_mx(hid_codes[:].bitcast(FP8X4), hid_scales[:], hid[:].rearrange("p j t -> p (j t)")),
                last_product,
                lambda: nc.scalar.copy(result[:], acc[:]),
                lambda: nc.sync.dma_start(out_rows[:, :, cols], result[:]),
            ]

        chunks = [chunk_steps(c) for c in range(len(CHUNKS))]
        n_steps = len(chunks[0])
        for tick in range(n_steps + LAG * (len(chunks) - 1)):
            for c, steps in enumerate(chunks):
                if 0 <= tick - LAG * c < n_steps:
                    steps[tick - LAG * c]()
